import numpy as np
import ml_dtypes


def mxq(x, axis, fmt="e4m3"):
    dtype, down = {"e4m3": (ml_dtypes.float8_e4m3fn, 7), "e5m2": (ml_dtypes.float8_e5m2, 14)}[fmt]
    v = np.moveaxis(np.asarray(x, np.float32).astype(ml_dtypes.bfloat16).astype(np.float64), axis, -1)
    blocks = v.reshape(v.shape[:-1] + (-1, 32))
    amax = np.abs(blocks).max(-1, keepdims=True)
    byte = np.maximum(np.where(amax > 0, np.frexp(amax)[1] - 1 + 127, 0) - down, 1)
    scale = np.exp2(byte - 127.0)
    codes = (blocks / scale).astype(np.float32).astype(dtype).astype(np.float64)
    return np.moveaxis((codes * scale).reshape(v.shape), -1, axis)


WIDE = False


def mx_kscale(k):
    if not WIDE:
        return np.ones(k)
    levels = np.array([10, -10, 5, -5, 0])
    if k % 512:
        return np.exp2(np.random.permutation(np.resize(levels, k // 32))).repeat(32)
    a = np.empty((k // 512, 16))
    for p in range(k // 512):
        a[p, :8] = np.random.permutation(np.resize(levels, 8))
        for g in range(8):
            far = levels[np.abs(levels - a[p, g]) >= 10]
            a[p, g + 8] = far[np.random.randint(len(far))]
    return np.exp2(a.ravel()).repeat(32)


BF16 = ml_dtypes.bfloat16


def bf(x):
    return np.asarray(x, np.float32).astype(BF16)


def f64(x):
    return np.asarray(x).astype(np.float64)


E2M1 = np.array([0.0, 0.5, 1.0, 1.5, 2.0, 3.0, 4.0, 6.0, -0.0, -0.5, -1.0, -1.5, -2.0, -3.0, -4.0, -6.0])


def pack_weight(w, fmt):
    k, n = w.shape
    w = f64(bf(w)).reshape(k // 32, 32, n)
    amax = np.abs(w).max(1)
    if fmt == "e4m3":
        byte = np.frexp(amax)[1] - 1 + 127 - 7
    else:
        mant, ex = np.frexp(amax / 6.0)
        byte = np.where(mant > 0.5, ex, ex - 1) + 127
    byte = np.clip(np.where(amax > 0, byte, 1), 1, 254)
    scaled = (w * np.exp2(127.0 - byte)[:, None, :]).reshape(k, n).astype(np.float32)
    by_word = np.ascontiguousarray(scaled.reshape(k // 512, 128, 4, n).transpose(0, 1, 3, 2))
    if fmt == "e4m3":
        words = by_word.astype(ml_dtypes.float8_e4m3fn).view(np.uint8)
    else:
        c = by_word.astype(ml_dtypes.float4_e2m1fn).view(np.uint8) & 0xF
        words = c[..., 0::2] | (c[..., 1::2] << 4)
    return np.ascontiguousarray(words), np.ascontiguousarray(byte.astype(np.uint8).reshape(k // 512, 16, n))


def unpack_weight(words, scales, fmt):
    g, p, n, _ = words.shape
    if fmt == "e4m3":
        vals = np.ascontiguousarray(words).view(ml_dtypes.float8_e4m3fn).astype(np.float64)
    else:
        nib = np.empty((g, p, n, 4), np.uint8)
        nib[..., 0::2] = words & 0xF
        nib[..., 1::2] = words >> 4
        vals = E2M1[nib]
    vals = vals * np.repeat(np.exp2(scales.astype(np.float64) - 127.0), 8, axis=1)[..., None]
    return vals.transpose(0, 1, 3, 2).reshape(g * 512, n)
def pack4(w):
    words, scales = pack_weight(w, "e2m1")
    return words.reshape(words.shape[0], 128, -1), scales


def unpack4(words, scales):
    return unpack_weight(words.reshape(words.shape[0], 128, -1, 2), scales, "e2m1")


E4M3FN = np.array([(-1.0 if i & 128 else 1.0) * ((1.0 + (i & 7) / 8.0) * 2.0 ** (((i >> 3) & 15) - 7) if i & 120 else (i & 7) * 2.0 ** -9) for i in range(256)])


def e4m3fn_bytes(y):
    return np.clip(np.asarray(y, np.float64), -448.0, 448.0).astype(np.float32).astype(ml_dtypes.float8_e4m3fn).view(np.uint8)


def e4m3fn_values(b):
    return E4M3FN[b]

def planes(Y):
    n, m = Y.shape
    b = f64(bf(Y)).reshape(n // 32, 32, m)
    amax = np.abs(b).max(1)
    byte = np.clip(np.where(amax > 0, np.frexp(amax)[1] - 1 + 127 - 7, 1), 1, 254)
    codes = (b * np.exp2(127.0 - byte)[:, None, :]).reshape(n, m).astype(np.float32).astype(ml_dtypes.float8_e4m3fn).view(np.uint8)
    words = codes.reshape(n // 512, 128, 4, m).transpose(0, 1, 3, 2)
    return np.ascontiguousarray(words), np.ascontiguousarray(byte.astype(np.uint8).reshape(n // 512, 16, m))


T, K, N, L, B = 2048, 1024, 1024, 4, 128
FP8_MAX = 448.0

def setup_inputs():
    s = mx_kscale(K)
    D = np.random.randn(L, K) / np.sqrt(K)
    U = np.random.randn(T, L) / np.sqrt(L)
    V = np.random.randn(N, L) / np.sqrt(L)
    points = (U[:, :, None] * D[None]).sum(axis=1) + 0.5 * np.random.randn(T, K) / np.sqrt(K)
    anchors = (V[:, :, None] * D[None]).sum(axis=1) + 0.5 * np.random.randn(N, K) / np.sqrt(K)
    xlen = (points ** 2).sum(axis=1, keepdims=True)
    alen = (anchors ** 2).sum(axis=1, keepdims=True).T
    X = points * s[None, :]
    X_scale = (np.abs(X).reshape(T, K // B, B).max(axis=2) / FP8_MAX).astype(np.float32)
    X_bytes = e4m3fn_bytes(X / np.repeat(f64(X_scale), B, axis=1))
    A_words, A_scales = pack4(anchors.T / s[:, None])
    mass = 2.0 * np.exp(0.8 * np.random.randn(1, N))
    return {"X_bytes": X_bytes, "X_scale": X_scale,
            "A_words": A_words, "A_scales": A_scales,
            "xlen": bf(xlen), "alen": bf(alen), "mass": bf(mass)}

def reference(X_bytes, X_scale, A_words, A_scales, xlen, alen, mass):
    X = e4m3fn_values(X_bytes) * np.repeat(f64(X_scale), B, axis=1)
    A = unpack4(A_words, A_scales)
    P = mxq(X, 1, "e4m3") @ A
    d2 = f64(xlen) + f64(alen) - 2.0 * P
    y = f64(mass) * (1.0 / (1.0 + d2))
    Y = y.T
    words, scales = planes(Y)
    return y, words, scales

@@ -1,0 +1,303 @@
+from contextlib import ExitStack
+
+import concourse.mybir as mybir
+from concourse.masks import make_identity
+
+T, K, N = 2048, 1024, 1024
+FLOPS = 2 * T * K * N
+
+F32 = mybir.dt.float32
+BF16 = mybir.dt.bfloat16
+I32 = mybir.dt.int32
+U32 = mybir.dt.uint32
+U8 = mybir.dt.uint8
+FP8 = mybir.dt.float8_e4m3fn
+FP8X4 = mybir.dt.float8_e4m3fn_x4
+FP4X4 = mybir.dt.float4_e2m1fn_x4
+ALU = mybir.AluOpType
+ACT = mybir.ActivationFunctionType
+
+P = 128
+CHUNK = 512
+TILES = T // P
+TILES_PER_CHUNK = CHUNK // P
+CHUNKS = T // CHUNK
+PASSES = K // 512
+GROUPS = N // 512
+BLOCKS = K // P
+STEPS = CHUNKS * GROUPS * 2
+
+
+def tile_anchor_layout_affinity_b2_kernel(
+    tc, X_bytes, X_scale, A_words, A_scales, xlen, alen, mass, out_0, out_1, out_2
+):
+    nc = tc.nc
+    with ExitStack() as ctx:
+        keep = ctx.enter_context(tc.tile_pool(name="keep", bufs=1))
+        work = ctx.enter_context(tc.tile_pool(name="work", bufs=3))
+        psum = ctx.enter_context(tc.psum_pool(name="psum", bufs=2))
+        ctx.enter_context(tc.manual_schedule())
+
+        a_words = keep.tile([P, PASSES, 2 * N], U8, align_bytes=64)
+        a_scales = keep.tile([P, PASSES, N], U8, align_bytes=64)
+        anchor_rows = keep.tile([P, P], BF16)
+        ident = keep.tile([P, P], F32)
+        ident_bf = keep.tile([P, P], BF16)
+        inv_mass = keep.tile([P, BLOCKS], F32)
+        offset = keep.tile([P, BLOCKS], F32)
+
+        nc.gpsimd.memset(anchor_rows[:], 0.0)
+        nc.gpsimd.memset(a_scales[:].rearrange("p g n -> p (g n)").bitcast(I32), 0)
+        make_identity(nc, ident[:])
+        make_identity(nc, ident_bf[:])
+
+        x_rows = X_bytes.rearrange("(i p) k -> p i k", p=P)
+        scale_rows = X_scale.rearrange("(i p) b -> p i b", p=P)
+        xlen_row = xlen.rearrange("t o -> (o t)")
+        x_raw = {}
+        x_scale = {}
+        xlen_b = {}
+
+        def load_bytes(first, count):
+            raw = keep.tile([P, count, K], U8, name="x_raw_%d" % first)
+            nc.sync.dma_start(out=raw[:], in_=x_rows[:, first : first + count, :])
+            for i in range(count):
+                x_raw[first + i] = raw[:, i, :]
+
+        def load_scales(first, count):
+            sc = keep.tile([P, count, BLOCKS], F32, name="x_scale_%d" % first)
+            nc.sync.dma_start(out=sc[:], in_=scale_rows[:, first : first + count, :])
+            for i in range(count):
+                x_scale[first + i] = sc[:, i, :]
+
+        def load_xlen(first, count):
+            row = keep.tile([P, count * CHUNK], BF16, name="xlen_b_%d" % first)
+            nc.sync.dma_start(
+                out=row[:], in_=xlen_row[first * CHUNK : (first + count) * CHUNK].partition_broadcast(P)
+            )
+            for c in range(count):
+                xlen_b[first + c] = row[:, c * CHUNK : (c + 1) * CHUNK]
+
+        load_bytes(0, 1)
+        load_scales(0, TILES_PER_CHUNK)
+        load_bytes(1, 1)
+        load_bytes(2, 2)
+        nc.scalar.dma_start(out=anchor_rows[0:BLOCKS, :], in_=alen.rearrange("o (j p) -> (o j) p", p=P))
+        nc.scalar.dma_start(
+            out=anchor_rows[BLOCKS : 2 * BLOCKS, :], in_=mass.rearrange("o (j p) -> (o j) p", p=P)
+        )
+        nc.sync.dma_start(out=a_words[:].bitcast(I32), in_=A_words.rearrange("g p b -> p g b").bitcast(I32))
+        for q in range(4):
+            nc.sync.dma_start(
+                out=a_scales[32 * q : 32 * q + 4, :, :].bitcast(I32),
+                in_=A_scales[:, 4 * q : 4 * q + 4, :].rearrange("g r n -> r g n").bitcast(I32),
+            )
+        load_xlen(0, 1)
+        load_scales(TILES_PER_CHUNK, TILES - TILES_PER_CHUNK)
+        load_bytes(4, 4)
+        load_xlen(1, CHUNKS - 1)
+        load_bytes(8, 4)
+        load_bytes(12, 4)
+
+        x_codes = [keep.tile([P, PASSES, CHUNK], U32, name="x_codes_%d" % c, align_bytes=64) for c in range(CHUNKS)]
+        x_mx = [keep.tile([P, PASSES, CHUNK], U8, name="x_mx_%d" % c, align_bytes=64) for c in range(CHUNKS)]
+        y_mx_early = keep.tile([P, GROUPS, T - CHUNK], U8, align_bytes=64)
+        y_mx_last = keep.tile([P, GROUPS, CHUNK], U8, align_bytes=64)
+
+        x_wide, x_bank, x_turned = {}, {}, {}
+        acc, u, r, r_bank, y, y_bf, y_bank, y_turned, y_codes = {}, {}, {}, {}, {}, {}, {}, {}, {}
+
+        def widen(i):
+            wide = work.tile([P, PASSES, 2, P, 2], BF16, name="x_wide")
+            x_wide[i] = wide
+            for b in range(BLOCKS):
+                g, q = divmod(b, 4)
+                nc.vector.tensor_scalar(
+                    out=wide[:, g, :, 32 * q : 32 * q + 32, :].rearrange("p u k e -> p k u e"),
+                    in0=x_raw[i][:, P * b : P * (b + 1)].bitcast(FP8).rearrange("p (k u e) -> p k u e", u=2, e=2),
+                    scalar1=x_scale[i][:, b : b + 1],
+                    scalar2=None,
+                    op0=ALU.mult,
+                )
+
+        def turn_x(i):
+            bank = psum.tile([P, PASSES, 2, P], F32, name="x_bank")
+            x_bank[i] = bank
+            words = x_wide[i][:].rearrange("p g u k e -> p (g u k e)").bitcast(F32)
+            for g in range(PASSES):
+                for h in range(2):
+                    s = 2 * g + h
+                    nc.tensor.transpose(bank[:, g, h, :], words[:, P * s : P * (s + 1)], ident[:])
+
+        def empty_x(i):
+            turned = work.tile([P, PASSES, P, 2], F32, name="x_turned", align_bytes=64)
+            x_turned[i] = turned
+            nc.scalar.copy(out=turned[:], in_=x_bank[i][:].rearrange("p g u m -> p g m u"))
+
+        def quantise_x(i):
+            c, ii = divmod(i, TILES_PER_CHUNK)
+            cols = slice(P * ii, P * (ii + 1))
+            for g in range(PASSES):
+                nc.vector.quantize_mx(
+                    out=x_codes[c][:, g, cols].bitcast(FP8X4),
+                    scales=x_mx[c][:, g, cols],
+                    in_=x_turned[i][:, g, :, :].rearrange("p m u -> p (m u)").bitcast(BF16),
+                )
+
+        def anchor_constants():
+            bank = psum.tile([P, P], BF16, name="y_bank")
+            nc.tensor.transpose(bank[:], anchor_rows[:], ident_bf[:])
+            nc.vector.reciprocal(out=inv_mass[:], in_=bank[:, BLOCKS : 2 * BLOCKS])
+            return bank
+
+        def anchor_offset(bank):
+            nc.vector.scalar_tensor_tensor(
+                out=offset[:], in0=bank[:, 0:BLOCKS], scalar=1.0, in1=inv_mass[:], op0=ALU.add, op1=ALU.mult
+            )
+
+        def multiply(s):
+            c = s // 4
+            for jj in range(2):
+                j = 2 * (s % 4) + jj
+                bank = psum.tile([P, CHUNK], F32, name="acc")
+                acc[s, jj] = bank
+                for g in range(PASSES):
+                    nc.tensor.matmul_mx(
+                        out=bank[:],
+                        lhsT=a_words[:, g, 2 * P * j : 2 * P * (j + 1)].bitcast(FP4X4),
+                        lhsT_scale=a_scales[:, g, P * j : P * (j + 1)],
+                        rhs=x_codes[c][:, g, :].bitcast(FP8X4),
+                        rhs_scale=x_mx[c][:, g, :],
+                        start=(g == 0),
+                        stop=(g == PASSES - 1),
+                    )
+
+        def add_xlen(s):
+            for jj in range(2):
+                part = work.tile([P, CHUNK], F32, name="u", bufs=4)
+                u[s, jj] = part
+                nc.vector.scalar_tensor_tensor(
+                    out=part[:], in0=acc[s, jj][:], scalar=-2.0, in1=xlen_b[s // 4], op0=ALU.mult, op1=ALU.add
+                )
+
+        def inverse_root(s):
+            for jj in range(2):
+                j = 2 * (s % 4) + jj
+                root = work.tile([P, CHUNK], F32, name="r", bufs=4)
+                r[s, jj] = root
+                nc.scalar.activation(
+                    out=root[:],
+                    in_=u[s, jj][:],
+                    func=ACT.Abs_reciprocal_sqrt,
+                    scale=inv_mass[:, j : j + 1],
+                    bias=offset[:, j : j + 1],
+                )
+
+        def turn_r(s):
+            for jj in range(2):
+                bank = psum.tile([P, TILES_PER_CHUNK, P], F32, name="r_bank")
+                r_bank[s, jj] = bank
+                for ii in range(TILES_PER_CHUNK):
+                    nc.tensor.transpose(bank[:, ii, :], r[s, jj][:, P * ii : P * (ii + 1)], ident[:])
+
+        def square(s):
+            res = work.tile([P, TILES_PER_CHUNK, 2 * P], F32, name="y", bufs=4)
+            y[s] = res
+            for jj in range(2):
+                nc.scalar.activation(out=res[:, :, P * jj : P * (jj + 1)], in_=r_bank[s, jj][:], func=ACT.Square)
+            c = s // 4
+            n0 = 2 * P * (s % 4)
+            rows = out_0[CHUNK * c : CHUNK * (c + 1), n0 : n0 + 2 * P]
+            nc.sync.dma_start(out=rows.rearrange("(i p) n -> p i n", p=P), in_=res[:])
+
+        def round_y(s):
+            grp, h = divmod(s, 2)
+            if h == 0:
+                y_bf[grp] = work.tile([P, TILES_PER_CHUNK, 2, P, 2], BF16, name="y_bf")
+            nc.vector.tensor_copy(
+                out=y_bf[grp][:, :, :, 64 * h : 64 * (h + 1), :],
+                in_=y[s][:].rearrange("p i (n u e) -> p i u n e", u=2, e=2),
+            )
+
+        def turn_y(s):
+            grp, h = divmod(s, 2)
+            bank = psum.tile([P, 2, 2, P], F32, name="y_bank")
+            y_bank[s] = bank
+            words = y_bf[grp][:].rearrange("p i u n e -> p (i u n e)").bitcast(F32)
+            for ii in range(2):
+                for hh in range(2):
+                    w = 4 * h + 2 * ii + hh
+                    nc.tensor.transpose(bank[:, ii, hh, :], words[:, P * w : P * (w + 1)], ident[:])
+
+        def empty_y(s):
+            turned = work.tile([P, 2, P, 2], F32, name="y_turned", align_bytes=64)
+            y_turned[s] = turned
+            src = y_bank[s][:].rearrange("p i u m -> p i m u")
+            if s % 2 == 0:
+                nc.scalar.copy(out=turned[:], in_=src)
+            else:
+                nc.vector.tensor_copy(out=turned[:], in_=src)
+
+        def quantise_y(s):
+            grp, h = divmod(s, 2)
+            c, g = divmod(grp, GROUPS)
+            if h == 0:
+                y_codes[grp] = work.tile([P, CHUNK], U32, name="y_codes", align_bytes=64)
+            if c < CHUNKS - 1:
+                plane, m0 = y_mx_early, CHUNK * c + 2 * P * h
+            else:
+                plane, m0 = y_mx_last, 2 * P * h
+            nc.vector.quantize_mx(
+                out=y_codes[grp][:, 2 * P * h : 2 * P * (h + 1)].bitcast(FP8X4),
+                scales=plane[:, g, m0 : m0 + 2 * P],
+                in_=y_turned[s][:].rearrange("p i m u -> p (i m u)").bitcast(BF16),
+            )
+            if h == 1:
+                dst = out_1[g].rearrange("p m t -> p (m t)")[:, 4 * CHUNK * c : 4 * CHUNK * (c + 1)]
+                nc.sync.dma_start(out=dst.bitcast(I32), in_=y_codes[grp][:].bitcast(I32))
+                if g == GROUPS - 1 and c >= CHUNKS - 2:
+                    cols = slice(0, T - CHUNK) if c == CHUNKS - 2 else slice(T - CHUNK, T)
+                    for q in range(4):
+                        nc.sync.dma_start(
+                            out=out_2[:, 4 * q : 4 * q + 4, cols].rearrange("g r m -> r g m").bitcast(I32),
+                            in_=plane[32 * q : 32 * q + 4, :, :].bitcast(I32),
+                        )
+
+        for i in range(TILES_PER_CHUNK):
+            widen(i)
+            turn_x(i)
+            empty_x(i)
+            if i >= 2:
+                quantise_x(i - 2)
+        bank0 = anchor_constants()
+        quantise_x(2)
+        anchor_offset(bank0)
+        quantise_x(3)
+
+        for s in range(STEPS + 6):
+            widened = [i for i in ([4, 5] if s == 0 else [s + 5]) if i < TILES]
+            quantised = [i for i in ([] if s == 0 else [4, 5] if s == 1 else [s + 4]) if i < TILES]
+            for i in widened:
+                widen(i)
+            if s < STEPS:
+                multiply(s)
+                add_xlen(s)
+                inverse_root(s)
+            if 0 <= s - 1 < STEPS:
+                turn_r(s - 1)
+            for i in widened:
+                turn_x(i)
+            if 0 <= s - 4 < STEPS:
+                turn_y(s - 4)
+            if 0 <= s - 1 < STEPS:
+                square(s - 1)
+            for i in widened:
+                empty_x(i)
+            for i in quantised:
+                quantise_x(i)
+            if 0 <= s - 5 < STEPS:
+                quantise_y(s - 5)
+            if 0 <= s - 2 < STEPS:
+                round_y(s - 2)
+            if 0 <= s - 4 < STEPS:
+                empty_y(s - 4)

@@ -26,6 +26,8 @@ PASSES = K // 512
 GROUPS = N // 512
 BLOCKS = K // P
 STEPS = CHUNKS * GROUPS * 2
+SCALAR_TILES = [4]
+EY_ACT = [0, 2, 4, 6, 8, 12, 13, 14]
 
 
 def tile_anchor_layout_affinity_b2_kernel(
@@ -40,20 +42,22 @@ def tile_anchor_layout_affinity_b2_kernel(
 
         a_words = keep.tile([P, PASSES, 2 * N], U8, align_bytes=64)
         a_scales = keep.tile([P, PASSES, N], U8, align_bytes=64)
-        anchor_rows = keep.tile([P, P], BF16)
+        vectors = keep.tile([P, P], BF16)
         ident = keep.tile([P, P], F32)
         ident_bf = keep.tile([P, P], BF16)
         inv_mass = keep.tile([P, BLOCKS], F32)
         offset = keep.tile([P, BLOCKS], F32)
+        xlen_col = keep.tile([P, TILES], BF16)
 
-        nc.gpsimd.memset(anchor_rows[:], 0.0)
+        warm = keep.tile([P, 2], F32)
+        nc.gpsimd.memset(warm[:, 0:1], 1.0)
+        nc.gpsimd.memset(vectors[:], 0.0)
         nc.gpsimd.memset(a_scales[:].rearrange("p g n -> p (g n)").bitcast(I32), 0)
         make_identity(nc, ident[:])
         make_identity(nc, ident_bf[:])
 
         x_rows = X_bytes.rearrange("(i p) k -> p i k", p=P)
         scale_rows = X_scale.rearrange("(i p) b -> p i b", p=P)
-        xlen_row = xlen.rearrange("t o -> (o t)")
         x_raw = {}
         x_scale = {}
         xlen_b = {}
@@ -70,67 +74,74 @@ def tile_anchor_layout_affinity_b2_kernel(
             for i in range(count):
                 x_scale[first + i] = sc[:, i, :]
 
-        def load_xlen(first, count):
-            row = keep.tile([P, count * CHUNK], BF16, name="xlen_b_%d" % first)
-            nc.sync.dma_start(
-                out=row[:], in_=xlen_row[first * CHUNK : (first + count) * CHUNK].partition_broadcast(P)
-            )
-            for c in range(count):
-                xlen_b[first + c] = row[:, c * CHUNK : (c + 1) * CHUNK]
+        def load_scales_early(first, count):
+            sc = keep.tile([P, count, BLOCKS], F32, name="x_scale_%d" % first)
+            nc.scalar.dma_start(out=sc[:], in_=scale_rows[:, first : first + count, :])
+            for i in range(count):
+                x_scale[first + i] = sc[:, i, :]
 
         load_bytes(0, 1)
-        load_scales(0, TILES_PER_CHUNK)
+        load_scales_early(0, TILES_PER_CHUNK)
         load_bytes(1, 1)
         load_bytes(2, 2)
-        nc.scalar.dma_start(out=anchor_rows[0:BLOCKS, :], in_=alen.rearrange("o (j p) -> (o j) p", p=P))
-        nc.scalar.dma_start(
-            out=anchor_rows[BLOCKS : 2 * BLOCKS, :], in_=mass.rearrange("o (j p) -> (o j) p", p=P)
-        )
+        nc.scalar.dma_start(out=vectors[0:BLOCKS, :], in_=alen.rearrange("o (j p) -> (o j) p", p=P))
+        nc.scalar.dma_start(out=vectors[BLOCKS : 2 * BLOCKS, :], in_=mass.rearrange("o (j p) -> (o j) p", p=P))
+        nc.scalar.dma_start(out=vectors[2 * BLOCKS : 2 * BLOCKS + TILES, :], in_=xlen.rearrange("(i p) o -> i (p o)", p=P))
+        nc.scalar.activation(out=warm[:, 1:2], in_=warm[:, 0:1], func=ACT.Abs_reciprocal_sqrt)
         nc.sync.dma_start(out=a_words[:].bitcast(I32), in_=A_words.rearrange("g p b -> p g b").bitcast(I32))
         for q in range(4):
             nc.sync.dma_start(
                 out=a_scales[32 * q : 32 * q + 4, :, :].bitcast(I32),
                 in_=A_scales[:, 4 * q : 4 * q + 4, :].rearrange("g r n -> r g n").bitcast(I32),
             )
-        load_xlen(0, 1)
-        load_scales(TILES_PER_CHUNK, TILES - TILES_PER_CHUNK)
+        load_scales(4, 4)
         load_bytes(4, 4)
-        load_xlen(1, CHUNKS - 1)
+        load_scales(8, 8)
         load_bytes(8, 4)
         load_bytes(12, 4)
 
         x_codes = [keep.tile([P, PASSES, CHUNK], U32, name="x_codes_%d" % c, align_bytes=64) for c in range(CHUNKS)]
         x_mx = [keep.tile([P, PASSES, CHUNK], U8, name="x_mx_%d" % c, align_bytes=64) for c in range(CHUNKS)]
-        y_mx_early = keep.tile([P, GROUPS, T - CHUNK], U8, align_bytes=64)
-        y_mx_last = keep.tile([P, GROUPS, CHUNK], U8, align_bytes=64)
+        y_mx = [keep.tile([P, GROUPS, T // 2], U8, name="y_mx_%d" % c, align_bytes=64) for c in range(2)]
 
+        done = set()
         x_wide, x_bank, x_turned = {}, {}, {}
         acc, u, r, r_bank, y, y_bf, y_bank, y_turned, y_codes = {}, {}, {}, {}, {}, {}, {}, {}, {}
 
         def widen(i):
-            wide = work.tile([P, PASSES, 2, P, 2], BF16, name="x_wide")
+            wide = work.tile([P, K], BF16, name="x_wide", bufs=4)
             x_wide[i] = wide
+            in_pairs = wide[:].rearrange("p (g u k e) -> p g k u e", g=PASSES, u=2, e=2)
             for b in range(BLOCKS):
                 g, q = divmod(b, 4)
-                nc.vector.tensor_scalar(
-                    out=wide[:, g, :, 32 * q : 32 * q + 32, :].rearrange("p u k e -> p k u e"),
-                    in0=x_raw[i][:, P * b : P * (b + 1)].bitcast(FP8).rearrange("p (k u e) -> p k u e", u=2, e=2),
-                    scalar1=x_scale[i][:, b : b + 1],
-                    scalar2=None,
-                    op0=ALU.mult,
-                )
+                codes = x_raw[i][:, P * b : P * (b + 1)].bitcast(FP8)
+                if i in SCALAR_TILES:
+                    nc.scalar.activation(
+                        out=wide[:, P * b : P * (b + 1)], in_=codes, func=ACT.Copy, scale=x_scale[i][:, b : b + 1]
+                    )
+                else:
+                    nc.vector.tensor_scalar(
+                        out=in_pairs[:, g, 32 * q : 32 * q + 32, :, :],
+                        in0=codes.rearrange("p (k u e) -> p k u e", u=2, e=2),
+                        scalar1=x_scale[i][:, b : b + 1],
+                        scalar2=None,
+                        op0=ALU.mult,
+                    )
 
         def turn_x(i):
-            bank = psum.tile([P, PASSES, 2, P], F32, name="x_bank")
+            bank = psum.tile([P, PASSES, 2, P], F32, name="t_bank", bufs=6)
             x_bank[i] = bank
-            words = x_wide[i][:].rearrange("p g u k e -> p (g u k e)").bitcast(F32)
+            words = x_wide[i][:].bitcast(F32)
             for g in range(PASSES):
                 for h in range(2):
-                    s = 2 * g + h
-                    nc.tensor.transpose(bank[:, g, h, :], words[:, P * s : P * (s + 1)], ident[:])
+                    if i in SCALAR_TILES:
+                        cols = slice(2 * P * g + h, 2 * P * (g + 1), 2)
+                    else:
+                        cols = slice(2 * P * g + P * h, 2 * P * g + P * (h + 1))
+                    nc.tensor.transpose(bank[:, g, h, :], words[:, cols], ident[:])
 
         def empty_x(i):
-            turned = work.tile([P, PASSES, P, 2], F32, name="x_turned", align_bytes=64)
+            turned = work.tile([P, PASSES, P, 2], F32, name="x_turned", align_bytes=64, bufs=4)
             x_turned[i] = turned
             nc.scalar.copy(out=turned[:], in_=x_bank[i][:].rearrange("p g u m -> p g m u"))
 
@@ -145,29 +156,39 @@ def tile_anchor_layout_affinity_b2_kernel(
                 )
 
         def anchor_constants():
-            bank = psum.tile([P, P], BF16, name="y_bank")
-            nc.tensor.transpose(bank[:], anchor_rows[:], ident_bf[:])
-            nc.vector.reciprocal(out=inv_mass[:], in_=bank[:, BLOCKS : 2 * BLOCKS])
+            bank = psum.tile([P, P], BF16, name="t_bank", bufs=6)
+            nc.tensor.transpose(bank[:], vectors[:], ident_bf[:])
             return bank
 
+        def spread_xlen(c):
+            bank = psum.tile([P, CHUNK], BF16, name="t_bank", bufs=6)
+            for ii in range(TILES_PER_CHUNK):
+                i = TILES_PER_CHUNK * c + ii
+                column = xlen_col[:, i : i + 1].to_broadcast([P, P])
+                nc.tensor.transpose(bank[:, P * ii : P * (ii + 1)], column, ident_bf[:])
+            row = keep.tile([P, CHUNK], BF16, name="xlen_b_%d" % c)
+            nc.scalar.copy(out=row[:], in_=bank[:])
+            xlen_b[c] = row[:]
+
         def anchor_offset(bank):
+            nc.vector.reciprocal(out=inv_mass[:], in_=bank[:, BLOCKS : 2 * BLOCKS])
             nc.vector.scalar_tensor_tensor(
                 out=offset[:], in0=bank[:, 0:BLOCKS], scalar=1.0, in1=inv_mass[:], op0=ALU.add, op1=ALU.mult
             )
 
-        def multiply(s):
+        def multiply(s, cols=slice(0, CHUNK)):
             c = s // 4
             for jj in range(2):
                 j = 2 * (s % 4) + jj
-                bank = psum.tile([P, CHUNK], F32, name="acc")
-                acc[s, jj] = bank
+                if cols.start == 0:
+                    acc[s, jj] = psum.tile([P, CHUNK], F32, name="acc")
                 for g in range(PASSES):
                     nc.tensor.matmul_mx(
-                        out=bank[:],
+                        out=acc[s, jj][:, cols],
                         lhsT=a_words[:, g, 2 * P * j : 2 * P * (j + 1)].bitcast(FP4X4),
                         lhsT_scale=a_scales[:, g, P * j : P * (j + 1)],
-                        rhs=x_codes[c][:, g, :].bitcast(FP8X4),
-                        rhs_scale=x_mx[c][:, g, :],
+                        rhs=x_codes[c][:, g, cols].bitcast(FP8X4),
+                        rhs_scale=x_mx[c][:, g, cols],
                         start=(g == 0),
                         stop=(g == PASSES - 1),
                     )
@@ -195,33 +216,33 @@ def tile_anchor_layout_affinity_b2_kernel(
 
         def turn_r(s):
             for jj in range(2):
-                bank = psum.tile([P, TILES_PER_CHUNK, P], F32, name="r_bank")
+                bank = psum.tile([P, TILES_PER_CHUNK, P], F32, name="t_bank", bufs=6)
                 r_bank[s, jj] = bank
                 for ii in range(TILES_PER_CHUNK):
                     nc.tensor.transpose(bank[:, ii, :], r[s, jj][:, P * ii : P * (ii + 1)], ident[:])
 
-        def square(s):
-            res = work.tile([P, TILES_PER_CHUNK, 2 * P], F32, name="y", bufs=4)
-            y[s] = res
-            for jj in range(2):
-                nc.scalar.activation(out=res[:, :, P * jj : P * (jj + 1)], in_=r_bank[s, jj][:], func=ACT.Square)
-            c = s // 4
-            n0 = 2 * P * (s % 4)
-            rows = out_0[CHUNK * c : CHUNK * (c + 1), n0 : n0 + 2 * P]
-            nc.sync.dma_start(out=rows.rearrange("(i p) n -> p i n", p=P), in_=res[:])
+        def square(s, jj):
+            if jj == 0:
+                y[s] = work.tile([P, TILES_PER_CHUNK, 2 * P], F32, name="y", bufs=4)
+            nc.scalar.activation(out=y[s][:, :, P * jj : P * (jj + 1)], in_=r_bank[s, jj][:], func=ACT.Square)
+            if jj == 1:
+                c = s // 4
+                n0 = 2 * P * (s % 4)
+                rows = out_0[CHUNK * c : CHUNK * (c + 1), n0 : n0 + 2 * P]
+                nc.sync.dma_start(out=rows.rearrange("(i p) n -> p i n", p=P), in_=y[s][:])
 
-        def round_y(s):
+        def round_y(s, lo=0, hi=64):
             grp, h = divmod(s, 2)
-            if h == 0:
+            if h == 0 and lo == 0:
                 y_bf[grp] = work.tile([P, TILES_PER_CHUNK, 2, P, 2], BF16, name="y_bf")
             nc.vector.tensor_copy(
-                out=y_bf[grp][:, :, :, 64 * h : 64 * (h + 1), :],
-                in_=y[s][:].rearrange("p i (n u e) -> p i u n e", u=2, e=2),
+                out=y_bf[grp][:, :, :, 64 * h + lo : 64 * h + hi, :],
+                in_=y[s][:, :, 4 * lo : 4 * hi].rearrange("p i (n u e) -> p i u n e", u=2, e=2),
             )
 
         def turn_y(s):
             grp, h = divmod(s, 2)
-            bank = psum.tile([P, 2, 2, P], F32, name="y_bank")
+            bank = psum.tile([P, 2, 2, P], F32, name="t_bank", bufs=6)
             y_bank[s] = bank
             words = y_bf[grp][:].rearrange("p i u n e -> p (i u n e)").bitcast(F32)
             for ii in range(2):
@@ -230,10 +251,10 @@ def tile_anchor_layout_affinity_b2_kernel(
                     nc.tensor.transpose(bank[:, ii, hh, :], words[:, P * w : P * (w + 1)], ident[:])
 
         def empty_y(s):
-            turned = work.tile([P, 2, P, 2], F32, name="y_turned", align_bytes=64)
+            turned = work.tile([P, 2, P, 2], F32, name="y_turned", align_bytes=64, bufs=4)
             y_turned[s] = turned
             src = y_bank[s][:].rearrange("p i u m -> p i m u")
-            if s % 2 == 0:
+            if s in EY_ACT:
                 nc.scalar.copy(out=turned[:], in_=src)
             else:
                 nc.vector.tensor_copy(out=turned[:], in_=src)
@@ -241,63 +262,100 @@ def tile_anchor_layout_affinity_b2_kernel(
         def quantise_y(s):
             grp, h = divmod(s, 2)
             c, g = divmod(grp, GROUPS)
-            if h == 0:
+            if grp not in y_codes:
                 y_codes[grp] = work.tile([P, CHUNK], U32, name="y_codes", align_bytes=64)
-            if c < CHUNKS - 1:
-                plane, m0 = y_mx_early, CHUNK * c + 2 * P * h
-            else:
-                plane, m0 = y_mx_last, 2 * P * h
+            plane, m0 = y_mx[c // 2], CHUNK * (c % 2) + 2 * P * h
             nc.vector.quantize_mx(
                 out=y_codes[grp][:, 2 * P * h : 2 * P * (h + 1)].bitcast(FP8X4),
                 scales=plane[:, g, m0 : m0 + 2 * P],
                 in_=y_turned[s][:].rearrange("p i m u -> p (i m u)").bitcast(BF16),
             )
-            if h == 1:
-                dst = out_1[g].rearrange("p m t -> p (m t)")[:, 4 * CHUNK * c : 4 * CHUNK * (c + 1)]
-                nc.sync.dma_start(out=dst.bitcast(I32), in_=y_codes[grp][:].bitcast(I32))
-                if g == GROUPS - 1 and c >= CHUNKS - 2:
-                    cols = slice(0, T - CHUNK) if c == CHUNKS - 2 else slice(T - CHUNK, T)
-                    for q in range(4):
-                        nc.sync.dma_start(
-                            out=out_2[:, 4 * q : 4 * q + 4, cols].rearrange("g r m -> r g m").bitcast(I32),
-                            in_=plane[32 * q : 32 * q + 4, :, :].bitcast(I32),
-                        )
+            done.add(s)
+            words_out = out_1[g].rearrange("p m t -> p (m t)").bitcast(I32)
+            if 2 * grp in done and 2 * grp + 1 in done:
+                nc.sync.dma_start(out=words_out[:, CHUNK * c : CHUNK * (c + 1)], in_=y_codes[grp][:].bitcast(I32))
+            if len(done) in (STEPS // 2, STEPS):
+                cols = slice(T // 2 * (c // 2), T // 2 * (c // 2 + 1))
+                for q in range(4):
+                    queue = nc.scalar if len(done) == STEPS and q >= 2 else nc.sync
+                    queue.dma_start(
+                        out=out_2[:, 4 * q : 4 * q + 4, cols].rearrange("g r m -> r g m").bitcast(I32),
+                        in_=plane[32 * q : 32 * q + 4, :, :].bitcast(I32),
+                    )
 
-        for i in range(TILES_PER_CHUNK):
-            widen(i)
-            turn_x(i)
-            empty_x(i)
-            if i >= 2:
-                quantise_x(i - 2)
+        widen(0)
+        turn_x(0)
+        empty_x(0)
+        widen(1)
+        turn_x(1)
         bank0 = anchor_constants()
-        quantise_x(2)
+        empty_x(1)
+        nc.scalar.copy(out=xlen_col[:], in_=bank0[:, 2 * BLOCKS : 2 * BLOCKS + TILES])
+        widen(2)
+        turn_x(2)
+        empty_x(2)
+        widen(3)
+        turn_x(3)
+        empty_x(3)
+        spread_xlen(0)
+        quantise_x(0)
+        quantise_x(1)
         anchor_offset(bank0)
+        quantise_x(2)
         quantise_x(3)
+        multiply(0)
 
-        for s in range(STEPS + 6):
+        last = STEPS - 1
+        for s in range(STEPS):
             widened = [i for i in ([4, 5] if s == 0 else [s + 5]) if i < TILES]
             quantised = [i for i in ([] if s == 0 else [4, 5] if s == 1 else [s + 4]) if i < TILES]
             for i in widened:
                 widen(i)
-            if s < STEPS:
+            if s > 0:
                 multiply(s)
-                add_xlen(s)
-                inverse_root(s)
-            if 0 <= s - 1 < STEPS:
+            add_xlen(s)
+            inverse_root(s)
+            if s >= 1:
                 turn_r(s - 1)
             for i in widened:
                 turn_x(i)
-            if 0 <= s - 4 < STEPS:
+            if s == 0:
+                spread_xlen(1)
+                spread_xlen(2)
+            if s == 1:
+                spread_xlen(3)
+            if s >= 4:
                 turn_y(s - 4)
-            if 0 <= s - 1 < STEPS:
-                square(s - 1)
+            if s >= 1:
+                square(s - 1, 0)
+                square(s - 1, 1)
             for i in widened:
                 empty_x(i)
             for i in quantised:
                 quantise_x(i)
-            if 0 <= s - 5 < STEPS:
+            if s >= 5:
                 quantise_y(s - 5)
-            if 0 <= s - 2 < STEPS:
+            if s >= 2:
                 round_y(s - 2)
-            if 0 <= s - 4 < STEPS:
+            if s >= 4:
                 empty_y(s - 4)
+
+        turn_r(last)
+        turn_y(last - 3)
+        turn_y(last - 2)
+        square(last, 0)
+        square(last, 1)
+        quantise_y(last - 4)
+        round_y(last - 1)
+        round_y(last, 0, 32)
+        round_y(last, 32, 64)
+        empty_y(last - 3)
+        empty_y(last - 2)
+        turn_y(last - 1)
+        turn_y(last)
+        quantise_y(last - 3)
+        empty_y(last)
+        empty_y(last - 1)
+        quantise_y(last - 2)
+        quantise_y(last)
+        quantise_y(last - 1)

@@ -27,7 +27,11 @@ GROUPS = N // 512
 BLOCKS = K // P
 STEPS = CHUNKS * GROUPS * 2
 SCALAR_TILES = [4]
-EY_ACT = [0, 2, 4, 6, 8, 12, 13, 14]
+EY_ACT = [12, 13, 14]
+POOL_STEPS = range(0, 14)
+EL = 5
+EX_DVE = [7, 8, 9]
+XL_DVE = []
 
 
 def tile_anchor_layout_affinity_b2_kernel(
@@ -50,11 +54,11 @@ def tile_anchor_layout_affinity_b2_kernel(
         xlen_col = keep.tile([P, TILES], BF16)
 
         warm = keep.tile([P, 2], F32)
-        nc.gpsimd.memset(warm[:, 0:1], 1.0)
-        nc.gpsimd.memset(vectors[:], 0.0)
-        nc.gpsimd.memset(a_scales[:].rearrange("p g n -> p (g n)").bitcast(I32), 0)
+        nc.vector.memset(vectors[:].bitcast(I32), 0)
+        nc.vector.memset(warm[:, 0:1], 1.0)
+        nc.vector.memset(a_scales[:].rearrange("p g n -> p (g n)").bitcast(I32), 0)
         make_identity(nc, ident[:])
-        make_identity(nc, ident_bf[:])
+        nc.vector.tensor_copy(out=ident_bf[:], in_=ident[:])
 
         x_rows = X_bytes.rearrange("(i p) k -> p i k", p=P)
         scale_rows = X_scale.rearrange("(i p) b -> p i b", p=P)
@@ -141,9 +145,13 @@ def tile_anchor_layout_affinity_b2_kernel(
                     nc.tensor.transpose(bank[:, g, h, :], words[:, cols], ident[:])
 
         def empty_x(i):
-            turned = work.tile([P, PASSES, P, 2], F32, name="x_turned", align_bytes=64, bufs=4)
+            turned = work.tile([P, PASSES, P, 2], F32, name="x_turned", align_bytes=64, bufs=5)
             x_turned[i] = turned
-            nc.scalar.copy(out=turned[:], in_=x_bank[i][:].rearrange("p g u m -> p g m u"))
+            src = x_bank[i][:].rearrange("p g u m -> p g m u")
+            if i in EX_DVE:
+                nc.vector.tensor_copy(out=turned[:], in_=src)
+            else:
+                nc.scalar.copy(out=turned[:], in_=src)
 
         def quantise_x(i):
             c, ii = divmod(i, TILES_PER_CHUNK)
@@ -167,7 +175,10 @@ def tile_anchor_layout_affinity_b2_kernel(
                 column = xlen_col[:, i : i + 1].to_broadcast([P, P])
                 nc.tensor.transpose(bank[:, P * ii : P * (ii + 1)], column, ident_bf[:])
             row = keep.tile([P, CHUNK], BF16, name="xlen_b_%d" % c)
-            nc.scalar.copy(out=row[:], in_=bank[:])
+            if c in XL_DVE:
+                nc.vector.tensor_copy(out=row[:], in_=bank[:])
+            else:
+                nc.scalar.copy(out=row[:], in_=bank[:])
             xlen_b[c] = row[:]
 
         def anchor_offset(bank):
@@ -176,30 +187,28 @@ def tile_anchor_layout_affinity_b2_kernel(
                 out=offset[:], in0=bank[:, 0:BLOCKS], scalar=1.0, in1=inv_mass[:], op0=ALU.add, op1=ALU.mult
             )
 
-        def multiply(s, cols=slice(0, CHUNK)):
+        def multiply(s, jj, cols=slice(0, CHUNK)):
             c = s // 4
-            for jj in range(2):
-                j = 2 * (s % 4) + jj
-                if cols.start == 0:
-                    acc[s, jj] = psum.tile([P, CHUNK], F32, name="acc")
-                for g in range(PASSES):
-                    nc.tensor.matmul_mx(
-                        out=acc[s, jj][:, cols],
-                        lhsT=a_words[:, g, 2 * P * j : 2 * P * (j + 1)].bitcast(FP4X4),
-                        lhsT_scale=a_scales[:, g, P * j : P * (j + 1)],
-                        rhs=x_codes[c][:, g, cols].bitcast(FP8X4),
-                        rhs_scale=x_mx[c][:, g, cols],
-                        start=(g == 0),
-                        stop=(g == PASSES - 1),
-                    )
-
-        def add_xlen(s):
-            for jj in range(2):
-                part = work.tile([P, CHUNK], F32, name="u", bufs=4)
-                u[s, jj] = part
-                nc.vector.scalar_tensor_tensor(
-                    out=part[:], in0=acc[s, jj][:], scalar=-2.0, in1=xlen_b[s // 4], op0=ALU.mult, op1=ALU.add
+            j = 2 * (s % 4) + jj
+            if cols.start == 0:
+                acc[s, jj] = psum.tile([P, CHUNK], F32, name="acc")
+            for g in range(PASSES):
+                nc.tensor.matmul_mx(
+                    out=acc[s, jj][:, cols],
+                    lhsT=a_words[:, g, 2 * P * j : 2 * P * (j + 1)].bitcast(FP4X4),
+                    lhsT_scale=a_scales[:, g, P * j : P * (j + 1)],
+                    rhs=x_codes[c][:, g, cols].bitcast(FP8X4),
+                    rhs_scale=x_mx[c][:, g, cols],
+                    start=(g == 0),
+                    stop=(g == PASSES - 1),
                 )
+
+        def add_xlen(s, jj):
+            part = work.tile([P, CHUNK], F32, name="u", bufs=4)
+            u[s, jj] = part
+            nc.vector.scalar_tensor_tensor(
+                out=part[:], in0=acc[s, jj][:], scalar=-2.0, in1=xlen_b[s // 4], op0=ALU.mult, op1=ALU.add
+            )
 
         def inverse_root(s):
             for jj in range(2):
@@ -235,10 +244,12 @@ def tile_anchor_layout_affinity_b2_kernel(
             grp, h = divmod(s, 2)
             if h == 0 and lo == 0:
                 y_bf[grp] = work.tile([P, TILES_PER_CHUNK, 2, P, 2], BF16, name="y_bf")
-            nc.vector.tensor_copy(
-                out=y_bf[grp][:, :, :, 64 * h + lo : 64 * h + hi, :],
-                in_=y[s][:, :, 4 * lo : 4 * hi].rearrange("p i (n u e) -> p i u n e", u=2, e=2),
-            )
+            dst = y_bf[grp][:, :, :, 64 * h + lo : 64 * h + hi, :].rearrange("p i u n e -> p u i n e")
+            src = y[s][:, :, 4 * lo : 4 * hi].rearrange("p i (n u e) -> p u i n e", u=2, e=2)
+            if s in POOL_STEPS:
+                nc.gpsimd.tensor_scalar(out=dst, in0=src, scalar1=1.0, scalar2=0.0, op0=ALU.mult, op1=ALU.add)
+            else:
+                nc.vector.tensor_copy(out=dst, in_=src)
 
         def turn_y(s):
             grp, h = divmod(s, 2)
@@ -303,50 +314,64 @@ def tile_anchor_layout_affinity_b2_kernel(
         anchor_offset(bank0)
         quantise_x(2)
         quantise_x(3)
-        multiply(0)
+        for i in range(TILES_PER_CHUNK):
+            multiply(0, 0, slice(P * i, P * (i + 1)))
+        multiply(0, 1)
 
         last = STEPS - 1
+        widen(4)
+        widen(5)
         for s in range(STEPS):
-            widened = [i for i in ([4, 5] if s == 0 else [s + 5]) if i < TILES]
-            quantised = [i for i in ([] if s == 0 else [4, 5] if s == 1 else [s + 4]) if i < TILES]
-            for i in widened:
-                widen(i)
+            turned = [i for i in ([4, 5, 6] if s == 0 else [s + 6]) if i < TILES]
+            quantised = [i for i in ([] if s == 0 else [4, 5, 6] if s == 1 else [s + 5]) if i < TILES]
             if s > 0:
-                multiply(s)
-            add_xlen(s)
+                multiply(s, 0)
+                multiply(s, 1)
+            add_xlen(s, 0)
+            add_xlen(s, 1)
+            if s == 0:
+                widen(6)
+            for i in quantised:
+                if i in EX_DVE:
+                    empty_x(i)
             inverse_root(s)
             if s >= 1:
                 turn_r(s - 1)
-            for i in widened:
+            for i in turned:
                 turn_x(i)
-            if s == 0:
-                spread_xlen(1)
-                spread_xlen(2)
-            if s == 1:
-                spread_xlen(3)
+            if s in (1, 2, 3):
+                spread_xlen(s)
             if s >= 4:
                 turn_y(s - 4)
+            if s >= EL:
+                empty_y(s - EL)
             if s >= 1:
                 square(s - 1, 0)
                 square(s - 1, 1)
-            for i in widened:
-                empty_x(i)
+                if s - 1 in POOL_STEPS:
+                    round_y(s - 1)
+            for i in turned:
+                if i not in EX_DVE:
+                    empty_x(i)
+            if s + 7 < TILES:
+                widen(s + 7)
             for i in quantised:
                 quantise_x(i)
-            if s >= 5:
-                quantise_y(s - 5)
-            if s >= 2:
+            if s >= EL:
+                quantise_y(s - EL)
+            if s >= 2 and s - 2 not in POOL_STEPS:
                 round_y(s - 2)
-            if s >= 4:
-                empty_y(s - 4)
 
         turn_r(last)
         turn_y(last - 3)
         turn_y(last - 2)
         square(last, 0)
         square(last, 1)
-        quantise_y(last - 4)
+        if EL == 5:
+            empty_y(last - 4)
         round_y(last - 1)
+        if EL == 5:
+            quantise_y(last - 4)
         round_y(last, 0, 32)
         round_y(last, 32, 64)
         empty_y(last - 3)

@@ -20,18 +20,23 @@ ACT = mybir.ActivationFunctionType
 P = 128
 CHUNK = 512
 TILES = T // P
-TILES_PER_CHUNK = CHUNK // P
+CHUNK_TILES = CHUNK // P
 CHUNKS = T // CHUNK
 PASSES = K // 512
 GROUPS = N // 512
-BLOCKS = K // P
-STEPS = CHUNKS * GROUPS * 2
-SCALAR_TILES = [4]
-EY_ACT = [12, 13, 14]
-POOL_STEPS = range(0, 14)
-EL = 5
-EX_DVE = [7, 8, 9]
-XL_DVE = []
+K_BLOCKS = K // P
+N_BLOCKS = N // P
+CHUNK_STEPS = N_BLOCKS // 2
+STEPS = CHUNKS * CHUNK_STEPS
+QUADRANTS = 4
+
+PRODUCT_BANKS = 2
+TURN_BANKS = 6
+
+TURN_Y_LAG = 4
+EMPTY_Y_LAG = 5
+
+SCALAR_TILE = CHUNK_TILES
 
 
 def tile_anchor_layout_affinity_b2_kernel(
@@ -41,19 +46,22 @@ def tile_anchor_layout_affinity_b2_kernel(
     with ExitStack() as ctx:
         keep = ctx.enter_context(tc.tile_pool(name="keep", bufs=1))
         work = ctx.enter_context(tc.tile_pool(name="work", bufs=3))
-        psum = ctx.enter_context(tc.psum_pool(name="psum", bufs=2))
+        psum = ctx.enter_context(tc.psum_pool(name="psum", bufs=PRODUCT_BANKS))
         ctx.enter_context(tc.manual_schedule())
 
         a_words = keep.tile([P, PASSES, 2 * N], U8, align_bytes=64)
         a_scales = keep.tile([P, PASSES, N], U8, align_bytes=64)
         vectors = keep.tile([P, P], BF16)
+        alen_rows = slice(0, N_BLOCKS)
+        mass_rows = slice(N_BLOCKS, 2 * N_BLOCKS)
+        xlen_rows = slice(2 * N_BLOCKS, 2 * N_BLOCKS + TILES)
         ident = keep.tile([P, P], F32)
         ident_bf = keep.tile([P, P], BF16)
-        inv_mass = keep.tile([P, BLOCKS], F32)
-        offset = keep.tile([P, BLOCKS], F32)
-        xlen_col = keep.tile([P, TILES], BF16)
-
+        inv_mass = keep.tile([P, N_BLOCKS], F32)
+        offset = keep.tile([P, N_BLOCKS], F32)
+        xlen_cols = keep.tile([P, TILES], BF16)
         warm = keep.tile([P, 2], F32)
+
         nc.vector.memset(vectors[:].bitcast(I32), 0)
         nc.vector.memset(warm[:, 0:1], 1.0)
         nc.vector.memset(a_scales[:].rearrange("p g n -> p (g n)").bitcast(I32), 0)
@@ -61,10 +69,8 @@ def tile_anchor_layout_affinity_b2_kernel(
         nc.vector.tensor_copy(out=ident_bf[:], in_=ident[:])
 
         x_rows = X_bytes.rearrange("(i p) k -> p i k", p=P)
-        scale_rows = X_scale.rearrange("(i p) b -> p i b", p=P)
-        x_raw = {}
-        x_scale = {}
-        xlen_b = {}
+        x_scale_rows = X_scale.rearrange("(i p) b -> p i b", p=P)
+        x_raw, x_scale = {}, {}
 
         def load_bytes(first, count):
             raw = keep.tile([P, count, K], U8, name="x_raw_%d" % first)
@@ -72,129 +78,109 @@ def tile_anchor_layout_affinity_b2_kernel(
             for i in range(count):
                 x_raw[first + i] = raw[:, i, :]
 
-        def load_scales(first, count):
-            sc = keep.tile([P, count, BLOCKS], F32, name="x_scale_%d" % first)
-            nc.sync.dma_start(out=sc[:], in_=scale_rows[:, first : first + count, :])
+        def load_x_scales(queue, first, count):
+            scales = keep.tile([P, count, K_BLOCKS], F32, name="x_scale_%d" % first)
+            queue.dma_start(out=scales[:], in_=x_scale_rows[:, first : first + count, :])
             for i in range(count):
-                x_scale[first + i] = sc[:, i, :]
-
-        def load_scales_early(first, count):
-            sc = keep.tile([P, count, BLOCKS], F32, name="x_scale_%d" % first)
-            nc.scalar.dma_start(out=sc[:], in_=scale_rows[:, first : first + count, :])
-            for i in range(count):
-                x_scale[first + i] = sc[:, i, :]
+                x_scale[first + i] = scales[:, i, :]
 
         load_bytes(0, 1)
-        load_scales_early(0, TILES_PER_CHUNK)
+        load_x_scales(nc.scalar, 0, CHUNK_TILES)
         load_bytes(1, 1)
         load_bytes(2, 2)
-        nc.scalar.dma_start(out=vectors[0:BLOCKS, :], in_=alen.rearrange("o (j p) -> (o j) p", p=P))
-        nc.scalar.dma_start(out=vectors[BLOCKS : 2 * BLOCKS, :], in_=mass.rearrange("o (j p) -> (o j) p", p=P))
-        nc.scalar.dma_start(out=vectors[2 * BLOCKS : 2 * BLOCKS + TILES, :], in_=xlen.rearrange("(i p) o -> i (p o)", p=P))
+        nc.scalar.dma_start(out=vectors[alen_rows, :], in_=alen.rearrange("o (j p) -> (o j) p", p=P))
+        nc.scalar.dma_start(out=vectors[mass_rows, :], in_=mass.rearrange("o (j p) -> (o j) p", p=P))
+        nc.scalar.dma_start(out=vectors[xlen_rows, :], in_=xlen.rearrange("(i p) o -> i (p o)", p=P))
         nc.scalar.activation(out=warm[:, 1:2], in_=warm[:, 0:1], func=ACT.Abs_reciprocal_sqrt)
         nc.sync.dma_start(out=a_words[:].bitcast(I32), in_=A_words.rearrange("g p b -> p g b").bitcast(I32))
-        for q in range(4):
+        for q in range(QUADRANTS):
             nc.sync.dma_start(
                 out=a_scales[32 * q : 32 * q + 4, :, :].bitcast(I32),
                 in_=A_scales[:, 4 * q : 4 * q + 4, :].rearrange("g r n -> r g n").bitcast(I32),
             )
-        load_scales(4, 4)
-        load_bytes(4, 4)
-        load_scales(8, 8)
-        load_bytes(8, 4)
-        load_bytes(12, 4)
+        load_x_scales(nc.sync, CHUNK_TILES, CHUNK_TILES)
+        load_bytes(CHUNK_TILES, CHUNK_TILES)
+        load_x_scales(nc.sync, 2 * CHUNK_TILES, 2 * CHUNK_TILES)
+        load_bytes(2 * CHUNK_TILES, CHUNK_TILES)
+        load_bytes(3 * CHUNK_TILES, CHUNK_TILES)
 
         x_codes = [keep.tile([P, PASSES, CHUNK], U32, name="x_codes_%d" % c, align_bytes=64) for c in range(CHUNKS)]
         x_mx = [keep.tile([P, PASSES, CHUNK], U8, name="x_mx_%d" % c, align_bytes=64) for c in range(CHUNKS)]
-        y_mx = [keep.tile([P, GROUPS, T // 2], U8, name="y_mx_%d" % c, align_bytes=64) for c in range(2)]
+        y_mx = [keep.tile([P, GROUPS, 2 * CHUNK], U8, name="y_mx_%d" % c, align_bytes=64) for c in range(CHUNKS // 2)]
 
-        done = set()
-        x_wide, x_bank, x_turned = {}, {}, {}
-        acc, u, r, r_bank, y, y_bf, y_bank, y_turned, y_codes = {}, {}, {}, {}, {}, {}, {}, {}, {}
+        x_wide, x_bank, x_turned, xlen_bank, xlen_spread = {}, {}, {}, {}, {}
+        product, u, r, r_bank, y, y_bf, y_bank, y_turned, y_codes = {}, {}, {}, {}, {}, {}, {}, {}, {}
+
+        def turn_bank(shape, dtype):
+            return psum.tile(shape, dtype, name="turn_bank", bufs=TURN_BANKS)
+
+        def copy_on(engine, out, in_):
+            if engine == "scalar":
+                nc.scalar.copy(out=out, in_=in_)
+            else:
+                nc.vector.tensor_copy(out=out, in_=in_)
 
         def widen(i):
-            wide = work.tile([P, K], BF16, name="x_wide", bufs=4)
-            x_wide[i] = wide
-            in_pairs = wide[:].rearrange("p (g u k e) -> p g k u e", g=PASSES, u=2, e=2)
-            for b in range(BLOCKS):
-                g, q = divmod(b, 4)
+            x_wide[i] = work.tile([P, K], BF16, name="x_wide", bufs=CHUNK_TILES)
+            in_pairs = x_wide[i][:].rearrange("m (g h p e) -> m g p h e", g=PASSES, h=2, e=2)
+            for b in range(K_BLOCKS):
                 codes = x_raw[i][:, P * b : P * (b + 1)].bitcast(FP8)
-                if i in SCALAR_TILES:
-                    nc.scalar.activation(
-                        out=wide[:, P * b : P * (b + 1)], in_=codes, func=ACT.Copy, scale=x_scale[i][:, b : b + 1]
-                    )
+                scale = x_scale[i][:, b : b + 1]
+                if i == SCALAR_TILE:
+                    nc.scalar.activation(out=x_wide[i][:, P * b : P * (b + 1)], in_=codes, func=ACT.Copy, scale=scale)
                 else:
+                    g, q = divmod(b, QUADRANTS)
                     nc.vector.tensor_scalar(
                         out=in_pairs[:, g, 32 * q : 32 * q + 32, :, :],
-                        in0=codes.rearrange("p (k u e) -> p k u e", u=2, e=2),
-                        scalar1=x_scale[i][:, b : b + 1],
+                        in0=codes.rearrange("m (p h e) -> m p h e", h=2, e=2),
+                        scalar1=scale,
                         scalar2=None,
                         op0=ALU.mult,
                     )
 
         def turn_x(i):
-            bank = psum.tile([P, PASSES, 2, P], F32, name="t_bank", bufs=6)
-            x_bank[i] = bank
-            words = x_wide[i][:].bitcast(F32)
+            x_bank[i] = turn_bank([P, PASSES, 2, P], F32)
+            pairs = x_wide[i][:].bitcast(F32)
             for g in range(PASSES):
                 for h in range(2):
-                    if i in SCALAR_TILES:
+                    if i == SCALAR_TILE:
                         cols = slice(2 * P * g + h, 2 * P * (g + 1), 2)
                     else:
                         cols = slice(2 * P * g + P * h, 2 * P * g + P * (h + 1))
-                    nc.tensor.transpose(bank[:, g, h, :], words[:, cols], ident[:])
+                    nc.tensor.transpose(x_bank[i][:, g, h, :], pairs[:, cols], ident[:])
 
-        def empty_x(i):
-            turned = work.tile([P, PASSES, P, 2], F32, name="x_turned", align_bytes=64, bufs=5)
-            x_turned[i] = turned
-            src = x_bank[i][:].rearrange("p g u m -> p g m u")
-            if i in EX_DVE:
-                nc.vector.tensor_copy(out=turned[:], in_=src)
-            else:
-                nc.scalar.copy(out=turned[:], in_=src)
+        def empty_x(i, engine):
+            x_turned[i] = work.tile([P, PASSES, P, 2], F32, name="x_turned", align_bytes=64, bufs=5)
+            copy_on(engine, x_turned[i][:], x_bank[i][:].rearrange("p g h m -> p g m h"))
 
         def quantise_x(i):
-            c, ii = divmod(i, TILES_PER_CHUNK)
-            cols = slice(P * ii, P * (ii + 1))
+            c, place = divmod(i, CHUNK_TILES)
+            cols = slice(P * place, P * (place + 1))
             for g in range(PASSES):
                 nc.vector.quantize_mx(
                     out=x_codes[c][:, g, cols].bitcast(FP8X4),
                     scales=x_mx[c][:, g, cols],
-                    in_=x_turned[i][:, g, :, :].rearrange("p m u -> p (m u)").bitcast(BF16),
+                    in_=x_turned[i][:, g, :, :].rearrange("p m h -> p (m h)").bitcast(BF16),
                 )
 
-        def anchor_constants():
-            bank = psum.tile([P, P], BF16, name="t_bank", bufs=6)
-            nc.tensor.transpose(bank[:], vectors[:], ident_bf[:])
-            return bank
-
         def spread_xlen(c):
-            bank = psum.tile([P, CHUNK], BF16, name="t_bank", bufs=6)
-            for ii in range(TILES_PER_CHUNK):
-                i = TILES_PER_CHUNK * c + ii
-                column = xlen_col[:, i : i + 1].to_broadcast([P, P])
-                nc.tensor.transpose(bank[:, P * ii : P * (ii + 1)], column, ident_bf[:])
-            row = keep.tile([P, CHUNK], BF16, name="xlen_b_%d" % c)
-            if c in XL_DVE:
-                nc.vector.tensor_copy(out=row[:], in_=bank[:])
-            else:
-                nc.scalar.copy(out=row[:], in_=bank[:])
-            xlen_b[c] = row[:]
+            xlen_bank[c] = turn_bank([P, CHUNK], BF16)
+            for place in range(CHUNK_TILES):
+                i = CHUNK_TILES * c + place
+                column = xlen_cols[:, i : i + 1].to_broadcast([P, P])
+                nc.tensor.transpose(xlen_bank[c][:, P * place : P * (place + 1)], column, ident_bf[:])
 
-        def anchor_offset(bank):
-            nc.vector.reciprocal(out=inv_mass[:], in_=bank[:, BLOCKS : 2 * BLOCKS])
-            nc.vector.scalar_tensor_tensor(
-                out=offset[:], in0=bank[:, 0:BLOCKS], scalar=1.0, in1=inv_mass[:], op0=ALU.add, op1=ALU.mult
-            )
+        def keep_xlen(c):
+            xlen_spread[c] = keep.tile([P, CHUNK], BF16, name="xlen_spread_%d" % c)
+            nc.scalar.copy(out=xlen_spread[c][:], in_=xlen_bank[c][:])
 
-        def multiply(s, jj, cols=slice(0, CHUNK)):
-            c = s // 4
-            j = 2 * (s % 4) + jj
+        def multiply(s, side, cols=slice(0, CHUNK)):
+            c, j = s // CHUNK_STEPS, 2 * (s % CHUNK_STEPS) + side
             if cols.start == 0:
-                acc[s, jj] = psum.tile([P, CHUNK], F32, name="acc")
+                product[s, side] = psum.tile([P, CHUNK], F32, name="product")
             for g in range(PASSES):
                 nc.tensor.matmul_mx(
-                    out=acc[s, jj][:, cols],
+                    out=product[s, side][:, cols],
                     lhsT=a_words[:, g, 2 * P * j : 2 * P * (j + 1)].bitcast(FP4X4),
                     lhsT_scale=a_scales[:, g, P * j : P * (j + 1)],
                     rhs=x_codes[c][:, g, cols].bitcast(FP8X4),
@@ -203,184 +189,196 @@ def tile_anchor_layout_affinity_b2_kernel(
                     stop=(g == PASSES - 1),
                 )
 
-        def add_xlen(s, jj):
-            part = work.tile([P, CHUNK], F32, name="u", bufs=4)
-            u[s, jj] = part
+        def add_xlen(s, side):
+            u[s, side] = work.tile([P, CHUNK], F32, name="u", bufs=4)
             nc.vector.scalar_tensor_tensor(
-                out=part[:], in0=acc[s, jj][:], scalar=-2.0, in1=xlen_b[s // 4], op0=ALU.mult, op1=ALU.add
+                out=u[s, side][:],
+                in0=product[s, side][:],
+                scalar=-2.0,
+                in1=xlen_spread[s // CHUNK_STEPS][:],
+                op0=ALU.mult,
+                op1=ALU.add,
             )
 
         def inverse_root(s):
-            for jj in range(2):
-                j = 2 * (s % 4) + jj
-                root = work.tile([P, CHUNK], F32, name="r", bufs=4)
-                r[s, jj] = root
+            for side in range(2):
+                j = 2 * (s % CHUNK_STEPS) + side
+                r[s, side] = work.tile([P, CHUNK], F32, name="r", bufs=4)
                 nc.scalar.activation(
-                    out=root[:],
-                    in_=u[s, jj][:],
+                    out=r[s, side][:],
+                    in_=u[s, side][:],
                     func=ACT.Abs_reciprocal_sqrt,
                     scale=inv_mass[:, j : j + 1],
                     bias=offset[:, j : j + 1],
                 )
 
         def turn_r(s):
-            for jj in range(2):
-                bank = psum.tile([P, TILES_PER_CHUNK, P], F32, name="t_bank", bufs=6)
-                r_bank[s, jj] = bank
-                for ii in range(TILES_PER_CHUNK):
-                    nc.tensor.transpose(bank[:, ii, :], r[s, jj][:, P * ii : P * (ii + 1)], ident[:])
+            for side in range(2):
+                r_bank[s, side] = turn_bank([P, CHUNK_TILES, P], F32)
+                for place in range(CHUNK_TILES):
+                    nc.tensor.transpose(
+                        r_bank[s, side][:, place, :], r[s, side][:, P * place : P * (place + 1)], ident[:]
+                    )
 
-        def square(s, jj):
-            if jj == 0:
-                y[s] = work.tile([P, TILES_PER_CHUNK, 2 * P], F32, name="y", bufs=4)
-            nc.scalar.activation(out=y[s][:, :, P * jj : P * (jj + 1)], in_=r_bank[s, jj][:], func=ACT.Square)
-            if jj == 1:
-                c = s // 4
-                n0 = 2 * P * (s % 4)
+        def square(s, side):
+            if side == 0:
+                y[s] = work.tile([P, CHUNK_TILES, 2 * P], F32, name="y", bufs=4)
+            nc.scalar.activation(out=y[s][:, :, P * side : P * (side + 1)], in_=r_bank[s, side][:], func=ACT.Square)
+            if side == 1:
+                c, n0 = s // CHUNK_STEPS, 2 * P * (s % CHUNK_STEPS)
                 rows = out_0[CHUNK * c : CHUNK * (c + 1), n0 : n0 + 2 * P]
-                nc.sync.dma_start(out=rows.rearrange("(i p) n -> p i n", p=P), in_=y[s][:])
+                nc.sync.dma_start(out=rows.rearrange("(i m) n -> m i n", m=P), in_=y[s][:])
 
-        def round_y(s, lo=0, hi=64):
-            grp, h = divmod(s, 2)
-            if h == 0 and lo == 0:
-                y_bf[grp] = work.tile([P, TILES_PER_CHUNK, 2, P, 2], BF16, name="y_bf")
-            dst = y_bf[grp][:, :, :, 64 * h + lo : 64 * h + hi, :].rearrange("p i u n e -> p u i n e")
-            src = y[s][:, :, 4 * lo : 4 * hi].rearrange("p i (n u e) -> p u i n e", u=2, e=2)
-            if s in POOL_STEPS:
+        def rounded_place(s, first, count):
+            if s % 2 == 0 and first == 0:
+                y_bf[s // 2] = work.tile([P, CHUNK_TILES, 2, P, 2], BF16, name="y_bf")
+            p0 = 64 * (s % 2) + first
+            return y_bf[s // 2][:, :, :, p0 : p0 + count, :].rearrange("m i h p e -> m h i p e")
+
+        def round_y(s, engine, count=64):
+            dst = rounded_place(s, 0, count)
+            src = y[s][:, :, 0 : 4 * count].rearrange("m i (p h e) -> m h i p e", h=2, e=2)
+            if engine == "gpsimd":
                 nc.gpsimd.tensor_scalar(out=dst, in0=src, scalar1=1.0, scalar2=0.0, op0=ALU.mult, op1=ALU.add)
             else:
                 nc.vector.tensor_copy(out=dst, in_=src)
 
-        def turn_y(s):
-            grp, h = divmod(s, 2)
-            bank = psum.tile([P, 2, 2, P], F32, name="t_bank", bufs=6)
-            y_bank[s] = bank
-            words = y_bf[grp][:].rearrange("p i u n e -> p (i u n e)").bitcast(F32)
-            for ii in range(2):
-                for hh in range(2):
-                    w = 4 * h + 2 * ii + hh
-                    nc.tensor.transpose(bank[:, ii, hh, :], words[:, P * w : P * (w + 1)], ident[:])
-
-        def empty_y(s):
-            turned = work.tile([P, 2, P, 2], F32, name="y_turned", align_bytes=64, bufs=4)
-            y_turned[s] = turned
-            src = y_bank[s][:].rearrange("p i u m -> p i m u")
-            if s in EY_ACT:
-                nc.scalar.copy(out=turned[:], in_=src)
-            else:
-                nc.vector.tensor_copy(out=turned[:], in_=src)
-
-        def quantise_y(s):
-            grp, h = divmod(s, 2)
-            c, g = divmod(grp, GROUPS)
-            if grp not in y_codes:
-                y_codes[grp] = work.tile([P, CHUNK], U32, name="y_codes", align_bytes=64)
-            plane, m0 = y_mx[c // 2], CHUNK * (c % 2) + 2 * P * h
-            nc.vector.quantize_mx(
-                out=y_codes[grp][:, 2 * P * h : 2 * P * (h + 1)].bitcast(FP8X4),
-                scales=plane[:, g, m0 : m0 + 2 * P],
-                in_=y_turned[s][:].rearrange("p i m u -> p (i m u)").bitcast(BF16),
+        def square_rounded(s):
+            nc.scalar.activation(
+                out=rounded_place(s, 32, 32),
+                in_=r_bank[s, 1][:].rearrange("m i (p h e) -> m h i p e", h=2, e=2),
+                func=ACT.Square,
             )
-            done.add(s)
-            words_out = out_1[g].rearrange("p m t -> p (m t)").bitcast(I32)
-            if 2 * grp in done and 2 * grp + 1 in done:
-                nc.sync.dma_start(out=words_out[:, CHUNK * c : CHUNK * (c + 1)], in_=y_codes[grp][:].bitcast(I32))
-            if len(done) in (STEPS // 2, STEPS):
-                cols = slice(T // 2 * (c // 2), T // 2 * (c // 2 + 1))
-                for q in range(4):
-                    queue = nc.scalar if len(done) == STEPS and q >= 2 else nc.sync
+
+        def turn_y(half):
+            y_bank[half] = turn_bank([P, 2, 2, P], F32)
+            pairs = y_bf[half // 2][:].rearrange("m i h p e -> m (i h p e)").bitcast(F32)
+            for place in range(2):
+                for h in range(2):
+                    block = 2 * (2 * (half % 2) + place) + h
+                    nc.tensor.transpose(y_bank[half][:, place, h, :], pairs[:, P * block : P * (block + 1)], ident[:])
+
+        def empty_y(half, engine):
+            y_turned[half] = work.tile([P, 2, P, 2], F32, name="y_turned", align_bytes=64, bufs=6)
+            copy_on(engine, y_turned[half][:], y_bank[half][:].rearrange("p i h m -> p i m h"))
+
+        def quantise_y(half):
+            c, g = divmod(half // 2, GROUPS)
+            m0 = 2 * P * (half % 2)
+            if half % 2 == 0:
+                y_codes[c, g] = work.tile([P, CHUNK], U32, name="y_codes", align_bytes=64)
+            scales, col0 = y_mx[c // 2], CHUNK * (c % 2) + m0
+            nc.vector.quantize_mx(
+                out=y_codes[c, g][:, m0 : m0 + 2 * P].bitcast(FP8X4),
+                scales=scales[:, g, col0 : col0 + 2 * P],
+                in_=y_turned[half][:].rearrange("p i m h -> p (i m h)").bitcast(BF16),
+            )
+            if half % 2 == 1:
+                words = out_1[g].rearrange("p m t -> p (m t)").bitcast(I32)
+                nc.sync.dma_start(out=words[:, CHUNK * c : CHUNK * (c + 1)], in_=y_codes[c, g][:].bitcast(I32))
+            if half % (2 * CHUNK_STEPS) == 2 * CHUNK_STEPS - 1:
+                cols = slice(CHUNK * (c - 1), CHUNK * (c + 1))
+                for q in range(QUADRANTS):
+                    queue = nc.scalar if half == STEPS - 1 and q >= QUADRANTS // 2 else nc.sync
                     queue.dma_start(
                         out=out_2[:, 4 * q : 4 * q + 4, cols].rearrange("g r m -> r g m").bitcast(I32),
-                        in_=plane[32 * q : 32 * q + 4, :, :].bitcast(I32),
+                        in_=scales[32 * q : 32 * q + 4, :, :].bitcast(I32),
                     )
 
-        widen(0)
-        turn_x(0)
-        empty_x(0)
-        widen(1)
-        turn_x(1)
-        bank0 = anchor_constants()
-        empty_x(1)
-        nc.scalar.copy(out=xlen_col[:], in_=bank0[:, 2 * BLOCKS : 2 * BLOCKS + TILES])
-        widen(2)
-        turn_x(2)
-        empty_x(2)
-        widen(3)
-        turn_x(3)
-        empty_x(3)
+        for i in range(CHUNK_TILES):
+            widen(i)
+            turn_x(i)
+            if i == 1:
+                vector_bank = turn_bank([P, P], BF16)
+                nc.tensor.transpose(vector_bank[:], vectors[:], ident_bf[:])
+            empty_x(i, "scalar")
+            if i == 1:
+                nc.scalar.copy(out=xlen_cols[:], in_=vector_bank[:, xlen_rows])
         spread_xlen(0)
+        keep_xlen(0)
         quantise_x(0)
         quantise_x(1)
-        anchor_offset(bank0)
+        nc.vector.reciprocal(out=inv_mass[:], in_=vector_bank[:, mass_rows])
+        nc.vector.scalar_tensor_tensor(
+            out=offset[:], in0=vector_bank[:, alen_rows], scalar=1.0, in1=inv_mass[:], op0=ALU.add, op1=ALU.mult
+        )
         quantise_x(2)
         quantise_x(3)
-        for i in range(TILES_PER_CHUNK):
+        for i in range(CHUNK_TILES):
             multiply(0, 0, slice(P * i, P * (i + 1)))
         multiply(0, 1)
+        widen(CHUNK_TILES)
+        widen(CHUNK_TILES + 1)
+
+        def tiles_turned(s):
+            if s < 2:
+                return [CHUNK_TILES + 2 * s, CHUNK_TILES + 2 * s + 1]
+            return [i for i in [2 * CHUNK_TILES + s - 2] if i < TILES]
+
+        def third_read(s):
+            return tiles_turned(s - 1)[-1] if 2 <= s < EMPTY_Y_LAG else None
 
         last = STEPS - 1
-        widen(4)
-        widen(5)
+        x_done = TILES - 2 * CHUNK_TILES + 3
         for s in range(STEPS):
-            turned = [i for i in ([4, 5, 6] if s == 0 else [s + 6]) if i < TILES]
-            quantised = [i for i in ([] if s == 0 else [4, 5, 6] if s == 1 else [s + 5]) if i < TILES]
             if s > 0:
                 multiply(s, 0)
                 multiply(s, 1)
             add_xlen(s, 0)
+            if s >= x_done:
+                quantise_y(s - EMPTY_Y_LAG - 1)
             add_xlen(s, 1)
             if s == 0:
-                widen(6)
-            for i in quantised:
-                if i in EX_DVE:
-                    empty_x(i)
+                widen(tiles_turned(1)[0])
+            if third_read(s) is not None:
+                empty_x(third_read(s), "vector")
             inverse_root(s)
+
             if s >= 1:
                 turn_r(s - 1)
-            for i in turned:
+            for i in tiles_turned(s):
                 turn_x(i)
-            if s in (1, 2, 3):
+            if 1 <= s < CHUNKS:
                 spread_xlen(s)
-            if s >= 4:
-                turn_y(s - 4)
-            if s >= EL:
-                empty_y(s - EL)
+            if s >= TURN_Y_LAG:
+                turn_y(s - TURN_Y_LAG)
+            if s >= EMPTY_Y_LAG:
+                empty_y(s - EMPTY_Y_LAG, "vector")
+
             if s >= 1:
                 square(s - 1, 0)
                 square(s - 1, 1)
-                if s - 1 in POOL_STEPS:
-                    round_y(s - 1)
-            for i in turned:
-                if i not in EX_DVE:
-                    empty_x(i)
-            if s + 7 < TILES:
-                widen(s + 7)
-            for i in quantised:
-                quantise_x(i)
-            if s >= EL:
-                quantise_y(s - EL)
-            if s >= 2 and s - 2 not in POOL_STEPS:
-                round_y(s - 2)
+                if s < last:
+                    round_y(s - 1, "gpsimd")
+            if 1 <= s < CHUNKS:
+                keep_xlen(s)
+            for i in tiles_turned(s):
+                if i != third_read(s + 1):
+                    empty_x(i, "scalar")
 
+            for i in tiles_turned(s + 1)[-1:]:
+                widen(i)
+            for i in tiles_turned(s - 1) if s >= 1 else []:
+                quantise_x(i)
+            if EMPTY_Y_LAG <= s < x_done - 1:
+                quantise_y(s - EMPTY_Y_LAG)
+
+        empty_y(last - 4, "vector")
         turn_r(last)
         turn_y(last - 3)
         turn_y(last - 2)
+        quantise_y(last - 5)
+        quantise_y(last - 4)
+        round_y(last - 1, "vector")
         square(last, 0)
+        square_rounded(last)
         square(last, 1)
-        if EL == 5:
-            empty_y(last - 4)
-        round_y(last - 1)
-        if EL == 5:
-            quantise_y(last - 4)
-        round_y(last, 0, 32)
-        round_y(last, 32, 64)
-        empty_y(last - 3)
-        empty_y(last - 2)
+        round_y(last, "vector", 32)
+        empty_y(last - 3, "vector")
+        empty_y(last - 2, "vector")
         turn_y(last - 1)
         turn_y(last)
-        quantise_y(last - 3)
-        empty_y(last)
-        empty_y(last - 1)
-        quantise_y(last - 2)
-        quantise_y(last)
-        quantise_y(last - 1)
+        empty_y(last - 1, "scalar")
+        empty_y(last, "scalar")
+        for half in range(last - 3, STEPS):
+            quantise_y(half)

from contextlib import ExitStack

import concourse.mybir as mybir
from concourse.masks import make_identity

T, K, N = 2048, 1024, 1024
FLOPS = 2 * T * K * N

F32 = mybir.dt.float32
BF16 = mybir.dt.bfloat16
I32 = mybir.dt.int32
U32 = mybir.dt.uint32
U8 = mybir.dt.uint8
FP8 = mybir.dt.float8_e4m3fn
FP8X4 = mybir.dt.float8_e4m3fn_x4
FP4X4 = mybir.dt.float4_e2m1fn_x4
ALU = mybir.AluOpType
ACT = mybir.ActivationFunctionType

P = 128
CHUNK = 512
TILES = T // P
CHUNK_TILES = CHUNK // P
CHUNKS = T // CHUNK
PASSES = K // 512
GROUPS = N // 512
K_BLOCKS = K // P
N_BLOCKS = N // P
CHUNK_STEPS = N_BLOCKS // 2
STEPS = CHUNKS * CHUNK_STEPS
QUADRANTS = 4

PRODUCT_BANKS = 2
TURN_BANKS = 6

TURN_Y_LAG = 4
EMPTY_Y_LAG = 5

SCALAR_TILE = CHUNK_TILES


def tile_anchor_layout_affinity_b2_kernel(
    tc, X_bytes, X_scale, A_words, A_scales, xlen, alen, mass, out_0, out_1, out_2
):
    nc = tc.nc
    with ExitStack() as ctx:
        keep = ctx.enter_context(tc.tile_pool(name="keep", bufs=1))
        work = ctx.enter_context(tc.tile_pool(name="work", bufs=3))
        psum = ctx.enter_context(tc.psum_pool(name="psum", bufs=PRODUCT_BANKS))
        ctx.enter_context(tc.manual_schedule())

        a_words = keep.tile([P, PASSES, 2 * N], U8, align_bytes=64)
        a_scales = keep.tile([P, PASSES, N], U8, align_bytes=64)
        vectors = keep.tile([P, P], BF16)
        alen_rows = slice(0, N_BLOCKS)
        mass_rows = slice(N_BLOCKS, 2 * N_BLOCKS)
        xlen_rows = slice(2 * N_BLOCKS, 2 * N_BLOCKS + TILES)
        ident = keep.tile([P, P], F32)
        ident_bf = keep.tile([P, P], BF16)
        inv_mass = keep.tile([P, N_BLOCKS], F32)
        offset = keep.tile([P, N_BLOCKS], F32)
        xlen_cols = keep.tile([P, TILES], BF16)
        warm = keep.tile([P, 2], F32)

        nc.vector.memset(vectors[:].bitcast(I32), 0)
        nc.vector.memset(warm[:, 0:1], 1.0)
        nc.vector.memset(a_scales[:].rearrange("p g n -> p (g n)").bitcast(I32), 0)
        make_identity(nc, ident[:])
        nc.vector.tensor_copy(out=ident_bf[:], in_=ident[:])

        x_rows = X_bytes.rearrange("(i p) k -> p i k", p=P)
        x_scale_rows = X_scale.rearrange("(i p) b -> p i b", p=P)
        x_raw, x_scale = {}, {}

        def load_bytes(first, count):
            raw = keep.tile([P, count, K], U8, name="x_raw_%d" % first)
            nc.sync.dma_start(out=raw[:], in_=x_rows[:, first : first + count, :])
            for i in range(count):
                x_raw[first + i] = raw[:, i, :]

        def load_x_scales(queue, first, count):
            scales = keep.tile([P, count, K_BLOCKS], F32, name="x_scale_%d" % first)
            queue.dma_start(out=scales[:], in_=x_scale_rows[:, first : first + count, :])
            for i in range(count):
                x_scale[first + i] = scales[:, i, :]

        load_bytes(0, 1)
        load_x_scales(nc.scalar, 0, CHUNK_TILES)
        load_bytes(1, 1)
        load_bytes(2, 2)
        nc.scalar.dma_start(out=vectors[alen_rows, :], in_=alen.rearrange("o (j p) -> (o j) p", p=P))
        nc.scalar.dma_start(out=vectors[mass_rows, :], in_=mass.rearrange("o (j p) -> (o j) p", p=P))
        nc.scalar.dma_start(out=vectors[xlen_rows, :], in_=xlen.rearrange("(i p) o -> i (p o)", p=P))
        nc.scalar.activation(out=warm[:, 1:2], in_=warm[:, 0:1], func=ACT.Abs_reciprocal_sqrt)
        nc.sync.dma_start(out=a_words[:].bitcast(I32), in_=A_words.rearrange("g p b -> p g b").bitcast(I32))
        for q in range(QUADRANTS):
            nc.sync.dma_start(
                out=a_scales[32 * q : 32 * q + 4, :, :].bitcast(I32),
                in_=A_scales[:, 4 * q : 4 * q + 4, :].rearrange("g r n -> r g n").bitcast(I32),
            )
        load_x_scales(nc.sync, CHUNK_TILES, CHUNK_TILES)
        load_bytes(CHUNK_TILES, CHUNK_TILES)
        load_x_scales(nc.sync, 2 * CHUNK_TILES, 2 * CHUNK_TILES)
        load_bytes(2 * CHUNK_TILES, CHUNK_TILES)
        load_bytes(3 * CHUNK_TILES, CHUNK_TILES)

        x_codes = [keep.tile([P, PASSES, CHUNK], U32, name="x_codes_%d" % c, align_bytes=64) for c in range(CHUNKS)]
        x_mx = [keep.tile([P, PASSES, CHUNK], U8, name="x_mx_%d" % c, align_bytes=64) for c in range(CHUNKS)]
        y_mx = [keep.tile([P, GROUPS, 2 * CHUNK], U8, name="y_mx_%d" % c, align_bytes=64) for c in range(CHUNKS // 2)]

        x_wide, x_bank, x_turned, xlen_bank, xlen_spread = {}, {}, {}, {}, {}
        product, u, r, r_bank, y, y_bf, y_bank, y_turned, y_codes = {}, {}, {}, {}, {}, {}, {}, {}, {}

        def turn_bank(shape, dtype):
            return psum.tile(shape, dtype, name="turn_bank", bufs=TURN_BANKS)

        def copy_on(engine, out, in_):
            if engine == "scalar":
                nc.scalar.copy(out=out, in_=in_)
            else:
                nc.vector.tensor_copy(out=out, in_=in_)

        def widen(i):
            x_wide[i] = work.tile([P, K], BF16, name="x_wide", bufs=CHUNK_TILES)
            in_pairs = x_wide[i][:].rearrange("m (g h p e) -> m g p h e", g=PASSES, h=2, e=2)
            for b in range(K_BLOCKS):
                codes = x_raw[i][:, P * b : P * (b + 1)].bitcast(FP8)
                scale = x_scale[i][:, b : b + 1]
                if i == SCALAR_TILE:
                    nc.scalar.activation(out=x_wide[i][:, P * b : P * (b + 1)], in_=codes, func=ACT.Copy, scale=scale)
                else:
                    g, q = divmod(b, QUADRANTS)
                    nc.vector.tensor_scalar(
                        out=in_pairs[:, g, 32 * q : 32 * q + 32, :, :],
                        in0=codes.rearrange("m (p h e) -> m p h e", h=2, e=2),
                        scalar1=scale,
                        scalar2=None,
                        op0=ALU.mult,
                    )

        def turn_x(i):
            x_bank[i] = turn_bank([P, PASSES, 2, P], F32)
            pairs = x_wide[i][:].bitcast(F32)
            for g in range(PASSES):
                for h in range(2):
                    if i == SCALAR_TILE:
                        cols = slice(2 * P * g + h, 2 * P * (g + 1), 2)
                    else:
                        cols = slice(2 * P * g + P * h, 2 * P * g + P * (h + 1))
                    nc.tensor.transpose(x_bank[i][:, g, h, :], pairs[:, cols], ident[:])

        def empty_x(i, engine):
            x_turned[i] = work.tile([P, PASSES, P, 2], F32, name="x_turned", align_bytes=64, bufs=5)
            copy_on(engine, x_turned[i][:], x_bank[i][:].rearrange("p g h m -> p g m h"))

        def quantise_x(i):
            c, place = divmod(i, CHUNK_TILES)
            cols = slice(P * place, P * (place + 1))
            for g in range(PASSES):
                nc.vector.quantize_mx(
                    out=x_codes[c][:, g, cols].bitcast(FP8X4),
                    scales=x_mx[c][:, g, cols],
                    in_=x_turned[i][:, g, :, :].rearrange("p m h -> p (m h)").bitcast(BF16),
                )

        def spread_xlen(c):
            xlen_bank[c] = turn_bank([P, CHUNK], BF16)
            for place in range(CHUNK_TILES):
                i = CHUNK_TILES * c + place
                column = xlen_cols[:, i : i + 1].to_broadcast([P, P])
                nc.tensor.transpose(xlen_bank[c][:, P * place : P * (place + 1)], column, ident_bf[:])

        def keep_xlen(c):
            xlen_spread[c] = keep.tile([P, CHUNK], BF16, name="xlen_spread_%d" % c)
            nc.scalar.copy(out=xlen_spread[c][:], in_=xlen_bank[c][:])

        def multiply(s, side, cols=slice(0, CHUNK)):
            c, j = s // CHUNK_STEPS, 2 * (s % CHUNK_STEPS) + side
            if cols.start == 0:
                product[s, side] = psum.tile([P, CHUNK], F32, name="product")
            for g in range(PASSES):
                nc.tensor.matmul_mx(
                    out=product[s, side][:, cols],
                    lhsT=a_words[:, g, 2 * P * j : 2 * P * (j + 1)].bitcast(FP4X4),
                    lhsT_scale=a_scales[:, g, P * j : P * (j + 1)],
                    rhs=x_codes[c][:, g, cols].bitcast(FP8X4),
                    rhs_scale=x_mx[c][:, g, cols],
                    start=(g == 0),
                    stop=(g == PASSES - 1),
                )

        def add_xlen(s, side):
            u[s, side] = work.tile([P, CHUNK], F32, name="u", bufs=4)
            nc.vector.scalar_tensor_tensor(
                out=u[s, side][:],
                in0=product[s, side][:],
                scalar=-2.0,
                in1=xlen_spread[s // CHUNK_STEPS][:],
                op0=ALU.mult,
                op1=ALU.add,
            )

        def inverse_root(s):
            for side in range(2):
                j = 2 * (s % CHUNK_STEPS) + side
                r[s, side] = work.tile([P, CHUNK], F32, name="r", bufs=4)
                nc.scalar.activation(
                    out=r[s, side][:],
                    in_=u[s, side][:],
                    func=ACT.Abs_reciprocal_sqrt,
                    scale=inv_mass[:, j : j + 1],
                    bias=offset[:, j : j + 1],
                )

        def turn_r(s):
            for side in range(2):
                r_bank[s, side] = turn_bank([P, CHUNK_TILES, P], F32)
                for place in range(CHUNK_TILES):
                    nc.tensor.transpose(
                        r_bank[s, side][:, place, :], r[s, side][:, P * place : P * (place + 1)], ident[:]
                    )

        def square(s, side):
            if side == 0:
                y[s] = work.tile([P, CHUNK_TILES, 2 * P], F32, name="y", bufs=4)
            nc.scalar.activation(out=y[s][:, :, P * side : P * (side + 1)], in_=r_bank[s, side][:], func=ACT.Square)
            if side == 1:
                c, n0 = s // CHUNK_STEPS, 2 * P * (s % CHUNK_STEPS)
                rows = out_0[CHUNK * c : CHUNK * (c + 1), n0 : n0 + 2 * P]
                nc.sync.dma_start(out=rows.rearrange("(i m) n -> m i n", m=P), in_=y[s][:])

        def rounded_place(s, first, count):
            if s % 2 == 0 and first == 0:
                y_bf[s // 2] = work.tile([P, CHUNK_TILES, 2, P, 2], BF16, name="y_bf")
            p0 = 64 * (s % 2) + first
            return y_bf[s // 2][:, :, :, p0 : p0 + count, :].rearrange("m i h p e -> m h i p e")

        def round_y(s, engine, count=64):
            dst = rounded_place(s, 0, count)
            src = y[s][:, :, 0 : 4 * count].rearrange("m i (p h e) -> m h i p e", h=2, e=2)
            if engine == "gpsimd":
                nc.gpsimd.tensor_scalar(out=dst, in0=src, scalar1=1.0, scalar2=0.0, op0=ALU.mult, op1=ALU.add)
            else:
                nc.vector.tensor_copy(out=dst, in_=src)

        def square_rounded(s):
            nc.scalar.activation(
                out=rounded_place(s, 32, 32),
                in_=r_bank[s, 1][:].rearrange("m i (p h e) -> m h i p e", h=2, e=2),
                func=ACT.Square,
            )

        def turn_y(half):
            y_bank[half] = turn_bank([P, 2, 2, P], F32)
            pairs = y_bf[half // 2][:].rearrange("m i h p e -> m (i h p e)").bitcast(F32)
            for place in range(2):
                for h in range(2):
                    block = 2 * (2 * (half % 2) + place) + h
                    nc.tensor.transpose(y_bank[half][:, place, h, :], pairs[:, P * block : P * (block + 1)], ident[:])

        def empty_y(half, engine):
            y_turned[half] = work.tile([P, 2, P, 2], F32, name="y_turned", align_bytes=64, bufs=6)
            copy_on(engine, y_turned[half][:], y_bank[half][:].rearrange("p i h m -> p i m h"))

        def quantise_y(half):
            c, g = divmod(half // 2, GROUPS)
            m0 = 2 * P * (half % 2)
            if half % 2 == 0:
                y_codes[c, g] = work.tile([P, CHUNK], U32, name="y_codes", align_bytes=64)
            scales, col0 = y_mx[c // 2], CHUNK * (c % 2) + m0
            nc.vector.quantize_mx(
                out=y_codes[c, g][:, m0 : m0 + 2 * P].bitcast(FP8X4),
                scales=scales[:, g, col0 : col0 + 2 * P],
                in_=y_turned[half][:].rearrange("p i m h -> p (i m h)").bitcast(BF16),
            )
            if half % 2 == 1:
                words = out_1[g].rearrange("p m t -> p (m t)").bitcast(I32)
                nc.sync.dma_start(out=words[:, CHUNK * c : CHUNK * (c + 1)], in_=y_codes[c, g][:].bitcast(I32))
            if half % (2 * CHUNK_STEPS) == 2 * CHUNK_STEPS - 1:
                cols = slice(CHUNK * (c - 1), CHUNK * (c + 1))
                for q in range(QUADRANTS):
                    queue = nc.scalar if half == STEPS - 1 and q >= QUADRANTS // 2 else nc.sync
                    queue.dma_start(
                        out=out_2[:, 4 * q : 4 * q + 4, cols].rearrange("g r m -> r g m").bitcast(I32),
                        in_=scales[32 * q : 32 * q + 4, :, :].bitcast(I32),
                    )

        for i in range(CHUNK_TILES):
            widen(i)
            turn_x(i)
            if i == 1:
                vector_bank = turn_bank([P, P], BF16)
                nc.tensor.transpose(vector_bank[:], vectors[:], ident_bf[:])
            empty_x(i, "scalar")
            if i == 1:
                nc.scalar.copy(out=xlen_cols[:], in_=vector_bank[:, xlen_rows])
        spread_xlen(0)
        keep_xlen(0)
        quantise_x(0)
        quantise_x(1)
        nc.vector.reciprocal(out=inv_mass[:], in_=vector_bank[:, mass_rows])
        nc.vector.scalar_tensor_tensor(
            out=offset[:], in0=vector_bank[:, alen_rows], scalar=1.0, in1=inv_mass[:], op0=ALU.add, op1=ALU.mult
        )
        quantise_x(2)
        quantise_x(3)
        for i in range(CHUNK_TILES):
            multiply(0, 0, slice(P * i, P * (i + 1)))
        multiply(0, 1)
        widen(CHUNK_TILES)
        widen(CHUNK_TILES + 1)

        def tiles_turned(s):
            if s < 2:
                return [CHUNK_TILES + 2 * s, CHUNK_TILES + 2 * s + 1]
            return [i for i in [2 * CHUNK_TILES + s - 2] if i < TILES]

        def third_read(s):
            return tiles_turned(s - 1)[-1] if 2 <= s < EMPTY_Y_LAG else None

        last = STEPS - 1
        x_done = TILES - 2 * CHUNK_TILES + 3
        for s in range(STEPS):
            if s > 0:
                multiply(s, 0)
                multiply(s, 1)
            add_xlen(s, 0)
            if s >= x_done:
                quantise_y(s - EMPTY_Y_LAG - 1)
            add_xlen(s, 1)
            if s == 0:
                widen(tiles_turned(1)[0])
            if third_read(s) is not None:
                empty_x(third_read(s), "vector")
            inverse_root(s)

            if s >= 1:
                turn_r(s - 1)
            for i in tiles_turned(s):
                turn_x(i)
            if 1 <= s < CHUNKS:
                spread_xlen(s)
            if s >= TURN_Y_LAG:
                turn_y(s - TURN_Y_LAG)
            if s >= EMPTY_Y_LAG:
                empty_y(s - EMPTY_Y_LAG, "vector")

            if s >= 1:
                square(s - 1, 0)
                square(s - 1, 1)
                if s < last:
                    round_y(s - 1, "gpsimd")
            if 1 <= s < CHUNKS:
                keep_xlen(s)
            for i in tiles_turned(s):
                if i != third_read(s + 1):
                    empty_x(i, "scalar")

            for i in tiles_turned(s + 1)[-1:]:
                widen(i)
            for i in tiles_turned(s - 1) if s >= 1 else []:
                quantise_x(i)
            if EMPTY_Y_LAG <= s < x_done - 1:
                quantise_y(s - EMPTY_Y_LAG)

        empty_y(last - 4, "vector")
        turn_r(last)
        turn_y(last - 3)
        turn_y(last - 2)
        quantise_y(last - 5)
        quantise_y(last - 4)
        round_y(last - 1, "vector")
        square(last, 0)
        square_rounded(last)
        square(last, 1)
        round_y(last, "vector", 32)
        empty_y(last - 3, "vector")
        empty_y(last - 2, "vector")
        turn_y(last - 1)
        turn_y(last)
        empty_y(last - 1, "scalar")
        empty_y(last, "scalar")
        for half in range(last - 3, STEPS):
            quantise_y(half)
